import numpy as np
import ml_dtypes


def mxq(x, axis, fmt="e4m3"):
    dtype, down = {"e4m3": (ml_dtypes.float8_e4m3fn, 7), "e5m2": (ml_dtypes.float8_e5m2, 14)}[fmt]
    v = np.moveaxis(np.asarray(x, np.float32).astype(ml_dtypes.bfloat16).astype(np.float64), axis, -1)
    blocks = v.reshape(v.shape[:-1] + (-1, 32))
    amax = np.abs(blocks).max(-1, keepdims=True)
    byte = np.maximum(np.where(amax > 0, np.frexp(amax)[1] - 1 + 127, 0) - down, 1)
    scale = np.exp2(byte - 127.0)
    codes = (blocks / scale).astype(np.float32).astype(dtype).astype(np.float64)
    return np.moveaxis((codes * scale).reshape(v.shape), -1, axis)


WIDE = False


def mx_kscale(k):
    if not WIDE:
        return np.ones(k)
    levels = np.array([10, -10, 5, -5, 0])
    if k % 512:
        return np.exp2(np.random.permutation(np.resize(levels, k // 32))).repeat(32)
    a = np.empty((k // 512, 16))
    for p in range(k // 512):
        a[p, :8] = np.random.permutation(np.resize(levels, 8))
        for g in range(8):
            far = levels[np.abs(levels - a[p, g]) >= 10]
            a[p, g + 8] = far[np.random.randint(len(far))]
    return np.exp2(a.ravel()).repeat(32)


def f64(x):
    return np.asarray(x).astype(np.float64)


def striped8(idx):
    return np.asarray(idx).reshape(8, -1, 16).transpose(0, 2, 1).reshape(128, -1).astype(np.uint16)


def unstriped8(offs):
    return offs.reshape(8, 16, -1).transpose(0, 2, 1).reshape(8, -1).astype(np.int64)


def pick8(x, idx, run):
    r = np.arange(len(x))
    return x[r[:, None], idx[r % (8 * run) // run]]


E2M1 = np.array([0.0, 0.5, 1.0, 1.5, 2.0, 3.0, 4.0, 6.0, -0.0, -0.5, -1.0, -1.5, -2.0, -3.0, -4.0, -6.0])


def pack_weight(w, fmt):
    k, n = w.shape
    w = f64(np.asarray(w, np.float32).astype(ml_dtypes.bfloat16)).reshape(k // 32, 32, n)
    amax = np.abs(w).max(1)
    if fmt == "e4m3":
        byte = np.frexp(amax)[1] - 1 + 127 - 7
    else:
        mant, ex = np.frexp(amax / 6.0)
        byte = np.where(mant > 0.5, ex, ex - 1) + 127
    byte = np.clip(np.where(amax > 0, byte, 1), 1, 254)
    scaled = (w * np.exp2(127.0 - byte)[:, None, :]).reshape(k, n).astype(np.float32)
    by_word = np.ascontiguousarray(scaled.reshape(k // 512, 128, 4, n).transpose(0, 1, 3, 2))
    if fmt == "e4m3":
        words = by_word.astype(ml_dtypes.float8_e4m3fn).view(np.uint8)
    else:
        c = by_word.astype(ml_dtypes.float4_e2m1fn).view(np.uint8) & 0xF
        words = (c[..., 0::2] | (c[..., 1::2] << 4)).reshape(k // 512, 128, 2 * n)
    return np.ascontiguousarray(words), np.ascontiguousarray(byte.astype(np.uint8).reshape(k // 512, 16, n))


def unpack_weight(words, scales, fmt):
    g, _, n = scales.shape
    words = np.ascontiguousarray(words).reshape(g, 128, n, -1)
    if fmt == "e4m3":
        vals = words.view(ml_dtypes.float8_e4m3fn).astype(np.float64)
    else:
        nib = np.empty((g, 128, n, 4), np.uint8)
        nib[..., 0::2] = words & 0xF
        nib[..., 1::2] = words >> 4
        vals = E2M1[nib]
    vals = vals * np.repeat(np.exp2(scales.astype(np.float64) - 127.0), 8, axis=1)[..., None]
    return vals.transpose(0, 1, 3, 2).reshape(g * 512, n)


def softplus(v):
    return np.log(1.0 + np.exp(v))


def sigmoid(v):
    return 1.0 / (1.0 + np.exp(-v))


D, E, T, Q, I = 512, 512, 1024, 128, 512


def setup_inputs():
    n = np.random.standard_normal
    idx = np.stack([np.random.permutation(T)[:I] for _ in range(8)])
    fd = mx_kscale(D)
    fe = mx_kscale(E)
    keysp = pack_weight(n((D, T)) / fd[:, None], "e2m1")
    return {
        "query": (n((D, Q)) * 1.0 / np.sqrt(D) * fd[:, None]).astype(np.float32),
        "keys_words": keysp[0],
        "keys_scales": keysp[1],
        "gout": (n((E, Q)) * 1 / np.sqrt(E) * fe[:, None]).astype(np.float32),
        "vals": (n((E, T)) / fe[:, None]).astype(np.float32),
        "th": (np.random.uniform(-0.5, 0.5, (Q, 1))).astype(np.float32),
        "reserve": (np.random.uniform(20.0, 60.0, (Q, 1))).astype(np.float32),
        "old": (0.5 * n((Q, T))).astype(np.float32),
        "offs": striped8(idx),
    }


def reference(query, keys_words, keys_scales, gout, vals, th, reserve, old, offs):
    idx = unstriped8(offs)
    keysu = unpack_weight(keys_words, keys_scales, "e2m1")
    queryq = mxq(f64(query), 0, "e4m3")
    a = queryq.T @ keysu
    p = softplus(pick8(a, idx, 16) - f64(th))
    z = np.sum(p, axis=1, keepdims=True) + f64(reserve)
    goutq = mxq(f64(gout), 0, "e4m3")
    valsq = mxq(f64(vals), 0, "e4m3")
    c0 = goutq.T @ valsq
    dw = pick8(c0, idx, 16)
    dz = np.sum(dw * p / np.square(z) * (-1.0), axis=1, keepdims=True)
    dp = dw / z + dz
    e1 = dp * sigmoid(pick8(a, idx, 16) - f64(th))
    s1 = np.zeros((Q, T))
    s1[np.arange(Q)[:, None], idx[np.arange(Q) % 128 // 16]] = e1
    y = s1 * 1024.0 + f64(old)
    return y

@@ -1,0 +1,171 @@
+from contextlib import ExitStack
+
+import concourse.mybir as mybir
+
+F32 = mybir.dt.float32
+BF16 = mybir.dt.bfloat16
+I32 = mybir.dt.int32
+U32 = mybir.dt.uint32
+U16 = mybir.dt.uint16
+U8 = mybir.dt.uint8
+FP8X4 = mybir.dt.float8_e4m3fn_x4
+FP4X4 = mybir.dt.float4_e2m1fn_x4
+ALU = mybir.AluOpType
+ACT = mybir.ActivationFunctionType
+
+P = 128
+PACK = 4
+T = 1024
+Q = 128
+SLOTS = 512
+GAIN = 1024.0
+FLOPS = 2 * 2 * 512 * Q * T
+
+SCORE_N = 256
+VAL_CHUNKS = (256, 256, 256, 128, 128)
+OUT_PIECES = (512, 512)
+
+
+def interleave(copy, grouped, raw):
+    copy(
+        out=grouped[:].rearrange("p (c i) j -> p c j i", i=4),
+        in_=raw[:].rearrange("p j (c i) -> p c j i", i=4),
+    )
+
+
+def tile_attend_bspotlight_heads_kernel(tc, query, keys_words, keys_scales, gout, vals, th, reserve, old, offs, out):
+    nc = tc.nc
+    with ExitStack() as ctx:
+        sb = ctx.enter_context(tc.tile_pool(name="sb", bufs=1))
+        psum = ctx.enter_context(tc.psum_pool(name="psum", bufs=8))
+
+        def load_rows(src, name):
+            raw = sb.tile([P, PACK, src.shape[1]], F32, name=name, align_bytes=64)
+            nc.sync.dma_start(out=raw[:], in_=src.rearrange("(p j) w -> p j w", j=PACK))
+            return raw
+
+        def quantise(copy, raw, name):
+            width = raw.shape[2]
+            grouped = sb.tile([P, width, PACK], BF16, name=name + "_bf", align_bytes=64)
+            interleave(copy, grouped, raw)
+            codes = sb.tile([P, width], U32, name=name + "_codes", align_bytes=64)
+            scales = sb.tile([P, width], U8, name=name + "_scales", align_bytes=64)
+            nc.vector.quantize_mx(
+                out=codes[:].bitcast(FP8X4),
+                scales=scales[:],
+                in_=grouped[:].rearrange("p w j -> p (w j)"),
+            )
+            return codes, scales
+
+        key_scales = sb.tile([P, T], U8, name="key_scales", align_bytes=64)
+        nc.vector.memset(key_scales[:].bitcast(U32), 0)
+        for quad in range(4):
+            nc.scalar.dma_start(
+                out=key_scales[32 * quad : 32 * quad + 4, :].bitcast(I32),
+                in_=keys_scales[0, 4 * quad : 4 * quad + 4, :].bitcast(I32),
+            )
+
+        q_raw = load_rows(query, "q_raw")
+        key_words = sb.tile([P, 2 * T], U8, name="key_words", align_bytes=64)
+        nc.sync.dma_start(out=key_words[:].bitcast(I32), in_=keys_words[0].bitcast(I32))
+        g_raw = load_rows(gout, "g_raw")
+        starts = [sum(VAL_CHUNKS[:c]) for c in range(len(VAL_CHUNKS))]
+        v_raw = [load_rows(vals[:, starts[0] : starts[0] + VAL_CHUNKS[0]], "v_raw0")]
+        offsets = sb.tile([P, SLOTS // 16], U16, name="offsets")
+        nc.sync.dma_start(offsets[:], offs)
+        for c in range(1, len(VAL_CHUNKS)):
+            v_raw.append(load_rows(vals[:, starts[c] : starts[c] + VAL_CHUNKS[c]], "v_raw%d" % c))
+        old_sb = sb.tile([P, T], F32, name="old_sb")
+        nc.sync.dma_start(out=old_sb[:], in_=old)
+
+        th_sb = sb.tile([P, 1], F32, name="th_sb")
+        nc.gpsimd.dma_start(out=th_sb[:], in_=th)
+        reserve_sb = sb.tile([P, 1], F32, name="reserve_sb")
+        nc.gpsimd.dma_start(out=reserve_sb[:], in_=reserve)
+        neg_th = sb.tile([P, 1], F32, name="neg_th")
+        nc.gpsimd.tensor_scalar(neg_th[:], th_sb[:], -1.0, 0.0, ALU.mult, ALU.add)
+
+        half = sb.tile([P, 1], F32, name="half")
+        nc.vector.memset(half[:], 0.5)
+        neg_half = sb.tile([P, 1], F32, name="neg_half")
+        nc.vector.memset(neg_half[:], -0.5)
+        placed = sb.tile([P, T], F32, name="placed")
+        nc.vector.memset(placed[:], 0.0)
+        warm = sb.tile([P, 1], F32, name="warm")
+        nc.scalar.activation(warm[:], half[:], ACT.Sigmoid)
+
+        q_codes, q_scales = quantise(nc.vector.tensor_copy, q_raw, "q")
+        scores = sb.tile([P, T], F32, name="scores")
+        for n, lo in enumerate(range(0, T, SCORE_N)):
+            bank = psum.tile([P, 512], F32, name="bank")
+            nc.tensor.matmul_mx(
+                out=bank[:, :SCORE_N],
+                lhsT=q_codes[:].bitcast(FP8X4),
+                lhsT_scale=q_scales[:],
+                rhs=key_words[:, 2 * lo : 2 * (lo + SCORE_N)].bitcast(FP4X4),
+                rhs_scale=key_scales[:, lo : lo + SCORE_N],
+                start=True,
+                stop=True,
+            )
+            copy = nc.vector.tensor_copy if n % 2 == 0 else nc.scalar.copy
+            copy(out=scores[:, lo : lo + SCORE_N], in_=bank[:, :SCORE_N])
+
+        g_codes, g_scales = quantise(nc.vector.tensor_copy, g_raw, "g")
+
+        picked = sb.tile([P, SLOTS], F32, name="picked")
+        nc.vector.tensor_copy(picked[:], scores[:].indirect(offsets[:]))
+        sig = sb.tile([P, SLOTS], F32, name="sig")
+        nc.scalar.activation(sig[:], picked[:], ACT.Sigmoid, bias=neg_th[:])
+        dist = sb.tile([P, SLOTS], F32, name="dist")
+        nc.scalar.activation(dist[:], sig[:], ACT.Abs, bias=neg_half[:])
+        log_sig = sb.tile([P, SLOTS], F32, name="log_sig")
+        nc.scalar.activation(log_sig[:], dist[:], ACT.Ln, bias=half[:])
+        relu = sb.tile([P, SLOTS], F32, name="relu")
+        nc.vector.tensor_scalar(relu[:], picked[:], th_sb[:], 0.0, ALU.subtract, ALU.max)
+
+        grads = sb.tile([P, T], F32, name="grads")
+        for c, width in enumerate(VAL_CHUNKS):
+            copy = nc.scalar.copy if c == 0 else nc.vector.tensor_copy
+            v_codes, v_scales = quantise(copy, v_raw[c], "v%d" % c)
+            bank = psum.tile([P, 512], F32, name="bank")
+            nc.tensor.matmul_mx(
+                out=bank[:, :width],
+                lhsT=g_codes[:].bitcast(FP8X4),
+                lhsT_scale=g_scales[:],
+                rhs=v_codes[:].bitcast(FP8X4),
+                rhs_scale=v_scales[:],
+                start=True,
+                stop=True,
+            )
+            nc.scalar.copy(out=grads[:, starts[c] : starts[c] + width], in_=bank[:, :width])
+
+        weight = sb.tile([P, SLOTS], F32, name="weight")
+        weight_sum = sb.tile([P, 1], F32, name="weight_sum")
+        nc.vector.scalar_tensor_tensor(
+            weight[:], relu[:], 1.0, log_sig[:], ALU.mult, ALU.subtract, accum_out=weight_sum[:]
+        )
+        neg_z = sb.tile([P, 1], F32, name="neg_z")
+        nc.vector.tensor_scalar(neg_z[:], weight_sum[:], reserve_sb[:], -1.0, ALU.add, ALU.mult)
+        neg_inv_z = sb.tile([P, 1], F32, name="neg_inv_z")
+        nc.vector.reciprocal(neg_inv_z[:], neg_z[:])
+        gain_z = sb.tile([P, 1], F32, name="gain_z")
+        nc.vector.tensor_scalar(gain_z[:], neg_inv_z[:], -GAIN, None, ALU.mult)
+
+        dw = sb.tile([P, SLOTS], F32, name="dw")
+        nc.vector.tensor_copy(dw[:], grads[:].indirect(offsets[:]))
+        terms = sb.tile([P, SLOTS], F32, name="terms")
+        shift = sb.tile([P, 1], F32, name="shift")
+        nc.vector.scalar_tensor_tensor(
+            terms[:], dw[:], neg_inv_z[:], weight[:], ALU.mult, ALU.mult, accum_out=shift[:]
+        )
+        dp = sb.tile([P, SLOTS], F32, name="dp")
+        nc.vector.tensor_scalar(dp[:], dw[:], shift[:], gain_z[:], ALU.add, ALU.mult)
+        nc.vector.tensor_tensor(placed[:].indirect(offsets[:]), dp[:], sig[:], ALU.mult)
+
+        lo = 0
+        for n, width in enumerate(OUT_PIECES):
+            piece = sb.tile([P, width], F32, name="piece%d" % n)
+            nc.vector.tensor_tensor(piece[:], placed[:, lo : lo + width], old_sb[:, lo : lo + width], ALU.add)
+            queue = nc.sync if n % 2 == 0 else nc.scalar
+            queue.dma_start(out=out[:, lo : lo + width], in_=piece[:])
+            lo = lo + width

@@ -22,8 +22,10 @@ GAIN = 1024.0
 FLOPS = 2 * 2 * 512 * Q * T
 
 SCORE_N = 256
-VAL_CHUNKS = (256, 256, 256, 128, 128)
-OUT_PIECES = (512, 512)
+VAL_CHUNKS = (256, 128, 256, 256, 128)
+BANK_CHUNKS = ((0, 1), (2, 3), (4,))
+HALF = SLOTS // 2
+OUT_PIECES = (512, 256, 256)
 
 
 def interleave(copy, grouped, raw):
@@ -58,32 +60,29 @@ def tile_attend_bspotlight_heads_kernel(tc, query, keys_words, keys_scales, gout
             return codes, scales
 
         key_scales = sb.tile([P, T], U8, name="key_scales", align_bytes=64)
-        nc.vector.memset(key_scales[:].bitcast(U32), 0)
-        for quad in range(4):
-            nc.scalar.dma_start(
-                out=key_scales[32 * quad : 32 * quad + 4, :].bitcast(I32),
-                in_=keys_scales[0, 4 * quad : 4 * quad + 4, :].bitcast(I32),
-            )
+        nc.gpsimd.memset(key_scales[:].bitcast(U32), 0)
 
+        offsets = sb.tile([P, SLOTS // 16], U16, name="offsets")
+        nc.sync.dma_start(offsets[:], offs)
+        th_sb = sb.tile([P, 1], F32, name="th_sb")
+        nc.sync.dma_start(out=th_sb[:], in_=th)
         q_raw = load_rows(query, "q_raw")
         key_words = sb.tile([P, 2 * T], U8, name="key_words", align_bytes=64)
         nc.sync.dma_start(out=key_words[:].bitcast(I32), in_=keys_words[0].bitcast(I32))
+        for quad in range(4):
+            nc.sync.dma_start(
+                out=key_scales[32 * quad : 32 * quad + 4, :].bitcast(I32),
+                in_=keys_scales[0, 4 * quad : 4 * quad + 4, :].bitcast(I32),
+            )
         g_raw = load_rows(gout, "g_raw")
         starts = [sum(VAL_CHUNKS[:c]) for c in range(len(VAL_CHUNKS))]
         v_raw = [load_rows(vals[:, starts[0] : starts[0] + VAL_CHUNKS[0]], "v_raw0")]
-        offsets = sb.tile([P, SLOTS // 16], U16, name="offsets")
-        nc.sync.dma_start(offsets[:], offs)
         for c in range(1, len(VAL_CHUNKS)):
             v_raw.append(load_rows(vals[:, starts[c] : starts[c] + VAL_CHUNKS[c]], "v_raw%d" % c))
+        reserve_sb = sb.tile([P, 1], F32, name="reserve_sb")
+        nc.sync.dma_start(out=reserve_sb[:], in_=reserve)
         old_sb = sb.tile([P, T], F32, name="old_sb")
         nc.sync.dma_start(out=old_sb[:], in_=old)
-
-        th_sb = sb.tile([P, 1], F32, name="th_sb")
-        nc.gpsimd.dma_start(out=th_sb[:], in_=th)
-        reserve_sb = sb.tile([P, 1], F32, name="reserve_sb")
-        nc.gpsimd.dma_start(out=reserve_sb[:], in_=reserve)
-        neg_th = sb.tile([P, 1], F32, name="neg_th")
-        nc.gpsimd.tensor_scalar(neg_th[:], th_sb[:], -1.0, 0.0, ALU.mult, ALU.add)
 
         half = sb.tile([P, 1], F32, name="half")
         nc.vector.memset(half[:], 0.5)
@@ -91,10 +90,13 @@ def tile_attend_bspotlight_heads_kernel(tc, query, keys_words, keys_scales, gout
         nc.vector.memset(neg_half[:], -0.5)
         placed = sb.tile([P, T], F32, name="placed")
         nc.vector.memset(placed[:], 0.0)
+        th_wide = sb.tile([P, SLOTS], F32, name="th_wide")
+        nc.gpsimd.tensor_scalar(th_wide[:], placed[:, :SLOTS], th_sb[:], 1.0, ALU.add, ALU.mult)
         warm = sb.tile([P, 1], F32, name="warm")
         nc.scalar.activation(warm[:], half[:], ACT.Sigmoid)
 
         q_codes, q_scales = quantise(nc.vector.tensor_copy, q_raw, "q")
+        g_codes, g_scales = quantise(nc.vector.tensor_copy, g_raw, "g")
         scores = sb.tile([P, T], F32, name="scores")
         for n, lo in enumerate(range(0, T, SCORE_N)):
             bank = psum.tile([P, 512], F32, name="bank")
@@ -107,52 +109,53 @@ def tile_attend_bspotlight_heads_kernel(tc, query, keys_words, keys_scales, gout
                 start=True,
                 stop=True,
             )
-            copy = nc.vector.tensor_copy if n % 2 == 0 else nc.scalar.copy
-            copy(out=scores[:, lo : lo + SCORE_N], in_=bank[:, :SCORE_N])
+            nc.scalar.copy(out=scores[:, lo : lo + SCORE_N], in_=bank[:, :SCORE_N])
 
-        g_codes, g_scales = quantise(nc.vector.tensor_copy, g_raw, "g")
-
-        picked = sb.tile([P, SLOTS], F32, name="picked")
-        nc.vector.tensor_copy(picked[:], scores[:].indirect(offsets[:]))
+        margin = sb.tile([P, SLOTS], F32, name="margin")
         sig = sb.tile([P, SLOTS], F32, name="sig")
-        nc.scalar.activation(sig[:], picked[:], ACT.Sigmoid, bias=neg_th[:])
         dist = sb.tile([P, SLOTS], F32, name="dist")
-        nc.scalar.activation(dist[:], sig[:], ACT.Abs, bias=neg_half[:])
+        for lo in range(0, SLOTS, HALF):
+            part = slice(lo, lo + HALF)
+            listed = offsets[:, lo // 16 : (lo + HALF) // 16]
+            nc.vector.tensor_tensor(margin[:, part], scores[:].indirect(listed), th_wide[:, part], ALU.subtract)
+            nc.scalar.activation(sig[:, part], margin[:, part], ACT.Sigmoid)
+            nc.scalar.activation(dist[:, part], sig[:, part], ACT.Abs, bias=neg_half[:])
         log_sig = sb.tile([P, SLOTS], F32, name="log_sig")
         nc.scalar.activation(log_sig[:], dist[:], ACT.Ln, bias=half[:])
-        relu = sb.tile([P, SLOTS], F32, name="relu")
-        nc.vector.tensor_scalar(relu[:], picked[:], th_sb[:], 0.0, ALU.subtract, ALU.max)
 
         grads = sb.tile([P, T], F32, name="grads")
-        for c, width in enumerate(VAL_CHUNKS):
-            copy = nc.scalar.copy if c == 0 else nc.vector.tensor_copy
-            v_codes, v_scales = quantise(copy, v_raw[c], "v%d" % c)
+        for chunks in BANK_CHUNKS:
             bank = psum.tile([P, 512], F32, name="bank")
-            nc.tensor.matmul_mx(
-                out=bank[:, :width],
-                lhsT=g_codes[:].bitcast(FP8X4),
-                lhsT_scale=g_scales[:],
-                rhs=v_codes[:].bitcast(FP8X4),
-                rhs_scale=v_scales[:],
-                start=True,
-                stop=True,
-            )
-            nc.scalar.copy(out=grads[:, starts[c] : starts[c] + width], in_=bank[:, :width])
+            first = starts[chunks[0]]
+            for c in chunks:
+                copy = nc.scalar.copy if c == 1 else nc.vector.tensor_copy
+                v_codes, v_scales = quantise(copy, v_raw[c], "v%d" % c)
+                nc.tensor.matmul_mx(
+                    out=bank[:, starts[c] - first : starts[c] - first + VAL_CHUNKS[c]],
+                    lhsT=g_codes[:].bitcast(FP8X4),
+                    lhsT_scale=g_scales[:],
+                    rhs=v_codes[:].bitcast(FP8X4),
+                    rhs_scale=v_scales[:],
+                    start=True,
+                    stop=True,
+                )
+            width = sum(VAL_CHUNKS[c] for c in chunks)
+            nc.scalar.copy(out=grads[:, first : first + width], in_=bank[:, :width])
 
+        dw = sb.tile([P, SLOTS], F32, name="dw")
+        nc.vector.tensor_copy(dw[:], grads[:].indirect(offsets[:]))
         weight = sb.tile([P, SLOTS], F32, name="weight")
         weight_sum = sb.tile([P, 1], F32, name="weight_sum")
         nc.vector.scalar_tensor_tensor(
-            weight[:], relu[:], 1.0, log_sig[:], ALU.mult, ALU.subtract, accum_out=weight_sum[:]
+            weight[:], margin[:], 0.0, log_sig[:], ALU.max, ALU.subtract, accum_out=weight_sum[:]
         )
         neg_z = sb.tile([P, 1], F32, name="neg_z")
         nc.vector.tensor_scalar(neg_z[:], weight_sum[:], reserve_sb[:], -1.0, ALU.add, ALU.mult)
         neg_inv_z = sb.tile([P, 1], F32, name="neg_inv_z")
         nc.vector.reciprocal(neg_inv_z[:], neg_z[:])
         gain_z = sb.tile([P, 1], F32, name="gain_z")
-        nc.vector.tensor_scalar(gain_z[:], neg_inv_z[:], -GAIN, None, ALU.mult)
+        nc.scalar.activation(gain_z[:], neg_inv_z[:], ACT.Copy, scale=-GAIN)
 
-        dw = sb.tile([P, SLOTS], F32, name="dw")
-        nc.vector.tensor_copy(dw[:], grads[:].indirect(offsets[:]))
         terms = sb.tile([P, SLOTS], F32, name="terms")
         shift = sb.tile([P, 1], F32, name="shift")
         nc.vector.scalar_tensor_tensor(

@@ -30,8 +30,8 @@ OUT_PIECES = (512, 256, 256)
 
 def interleave(copy, grouped, raw):
     copy(
-        out=grouped[:].rearrange("p (c i) j -> p c j i", i=4),
-        in_=raw[:].rearrange("p j (c i) -> p c j i", i=4),
+        out=grouped[:],
+        in_=raw[:].rearrange("p j w -> p w j"),
     )
 
 
@@ -84,16 +84,12 @@ def tile_attend_bspotlight_heads_kernel(tc, query, keys_words, keys_scales, gout
         old_sb = sb.tile([P, T], F32, name="old_sb")
         nc.sync.dma_start(out=old_sb[:], in_=old)
 
-        half = sb.tile([P, 1], F32, name="half")
-        nc.vector.memset(half[:], 0.5)
-        neg_half = sb.tile([P, 1], F32, name="neg_half")
-        nc.vector.memset(neg_half[:], -0.5)
         placed = sb.tile([P, T], F32, name="placed")
         nc.vector.memset(placed[:], 0.0)
         th_wide = sb.tile([P, SLOTS], F32, name="th_wide")
         nc.gpsimd.tensor_scalar(th_wide[:], placed[:, :SLOTS], th_sb[:], 1.0, ALU.add, ALU.mult)
-        warm = sb.tile([P, 1], F32, name="warm")
-        nc.scalar.activation(warm[:], half[:], ACT.Sigmoid)
+        half = sb.tile([P, 1], F32, name="half")
+        nc.scalar.activation(half[:], placed[:, 0:1], ACT.Sigmoid)
 
         q_codes, q_scales = quantise(nc.vector.tensor_copy, q_raw, "q")
         g_codes, g_scales = quantise(nc.vector.tensor_copy, g_raw, "g")
@@ -113,17 +109,17 @@ def tile_attend_bspotlight_heads_kernel(tc, query, keys_words, keys_scales, gout
 
         margin = sb.tile([P, SLOTS], F32, name="margin")
         sig = sb.tile([P, SLOTS], F32, name="sig")
-        dist = sb.tile([P, SLOTS], F32, name="dist")
+        dist = sb.tile([P, SLOTS], F32, name="dist", tag="dist_grads")
         for lo in range(0, SLOTS, HALF):
             part = slice(lo, lo + HALF)
             listed = offsets[:, lo // 16 : (lo + HALF) // 16]
             nc.vector.tensor_tensor(margin[:, part], scores[:].indirect(listed), th_wide[:, part], ALU.subtract)
             nc.scalar.activation(sig[:, part], margin[:, part], ACT.Sigmoid)
-            nc.scalar.activation(dist[:, part], sig[:, part], ACT.Abs, bias=neg_half[:])
+            nc.scalar.activation(dist[:, part], sig[:, part], ACT.Abs, bias=half[:], scale=-1.0)
         log_sig = sb.tile([P, SLOTS], F32, name="log_sig")
         nc.scalar.activation(log_sig[:], dist[:], ACT.Ln, bias=half[:])
 
-        grads = sb.tile([P, T], F32, name="grads")
+        grads = sb.tile([P, T], F32, name="grads", tag="dist_grads")
         for chunks in BANK_CHUNKS:
             bank = psum.tile([P, 512], F32, name="bank")
             first = starts[chunks[0]]
@@ -142,8 +138,6 @@ def tile_attend_bspotlight_heads_kernel(tc, query, keys_words, keys_scales, gout
             width = sum(VAL_CHUNKS[c] for c in chunks)
             nc.scalar.copy(out=grads[:, first : first + width], in_=bank[:, :width])
 
-        dw = sb.tile([P, SLOTS], F32, name="dw")
-        nc.vector.tensor_copy(dw[:], grads[:].indirect(offsets[:]))
         weight = sb.tile([P, SLOTS], F32, name="weight")
         weight_sum = sb.tile([P, 1], F32, name="weight_sum")
         nc.vector.scalar_tensor_tensor(
@@ -156,6 +150,8 @@ def tile_attend_bspotlight_heads_kernel(tc, query, keys_words, keys_scales, gout
         gain_z = sb.tile([P, 1], F32, name="gain_z")
         nc.scalar.activation(gain_z[:], neg_inv_z[:], ACT.Copy, scale=-GAIN)
 
+        dw = sb.tile([P, SLOTS], F32, name="dw")
+        nc.vector.tensor_copy(dw[:], grads[:].indirect(offsets[:]))
         terms = sb.tile([P, SLOTS], F32, name="terms")
         shift = sb.tile([P, 1], F32, name="shift")
         nc.vector.scalar_tensor_tensor(

from contextlib import ExitStack

import concourse.mybir as mybir

F32 = mybir.dt.float32
BF16 = mybir.dt.bfloat16
I32 = mybir.dt.int32
U32 = mybir.dt.uint32
U16 = mybir.dt.uint16
U8 = mybir.dt.uint8
FP8X4 = mybir.dt.float8_e4m3fn_x4
FP4X4 = mybir.dt.float4_e2m1fn_x4
ALU = mybir.AluOpType
ACT = mybir.ActivationFunctionType

P = 128
PACK = 4
T = 1024
Q = 128
SLOTS = 512
GAIN = 1024.0
FLOPS = 2 * 2 * 512 * Q * T

SCORE_N = 256
VAL_CHUNKS = (256, 128, 256, 256, 128)
BANK_CHUNKS = ((0, 1), (2, 3), (4,))
HALF = SLOTS // 2
OUT_PIECES = (512, 256, 256)


def interleave(copy, grouped, raw):
    copy(
        out=grouped[:],
        in_=raw[:].rearrange("p j w -> p w j"),
    )


def tile_attend_bspotlight_heads_kernel(tc, query, keys_words, keys_scales, gout, vals, th, reserve, old, offs, out):
    nc = tc.nc
    with ExitStack() as ctx:
        sb = ctx.enter_context(tc.tile_pool(name="sb", bufs=1))
        psum = ctx.enter_context(tc.psum_pool(name="psum", bufs=8))

        def load_rows(src, name):
            raw = sb.tile([P, PACK, src.shape[1]], F32, name=name, align_bytes=64)
            nc.sync.dma_start(out=raw[:], in_=src.rearrange("(p j) w -> p j w", j=PACK))
            return raw

        def quantise(copy, raw, name):
            width = raw.shape[2]
            grouped = sb.tile([P, width, PACK], BF16, name=name + "_bf", align_bytes=64)
            interleave(copy, grouped, raw)
            codes = sb.tile([P, width], U32, name=name + "_codes", align_bytes=64)
            scales = sb.tile([P, width], U8, name=name + "_scales", align_bytes=64)
            nc.vector.quantize_mx(
                out=codes[:].bitcast(FP8X4),
                scales=scales[:],
                in_=grouped[:].rearrange("p w j -> p (w j)"),
            )
            return codes, scales

        key_scales = sb.tile([P, T], U8, name="key_scales", align_bytes=64)
        nc.gpsimd.memset(key_scales[:].bitcast(U32), 0)

        offsets = sb.tile([P, SLOTS // 16], U16, name="offsets")
        nc.sync.dma_start(offsets[:], offs)
        th_sb = sb.tile([P, 1], F32, name="th_sb")
        nc.sync.dma_start(out=th_sb[:], in_=th)
        q_raw = load_rows(query, "q_raw")
        key_words = sb.tile([P, 2 * T], U8, name="key_words", align_bytes=64)
        nc.sync.dma_start(out=key_words[:].bitcast(I32), in_=keys_words[0].bitcast(I32))
        for quad in range(4):
            nc.sync.dma_start(
                out=key_scales[32 * quad : 32 * quad + 4, :].bitcast(I32),
                in_=keys_scales[0, 4 * quad : 4 * quad + 4, :].bitcast(I32),
            )
        g_raw = load_rows(gout, "g_raw")
        starts = [sum(VAL_CHUNKS[:c]) for c in range(len(VAL_CHUNKS))]
        v_raw = [load_rows(vals[:, starts[0] : starts[0] + VAL_CHUNKS[0]], "v_raw0")]
        for c in range(1, len(VAL_CHUNKS)):
            v_raw.append(load_rows(vals[:, starts[c] : starts[c] + VAL_CHUNKS[c]], "v_raw%d" % c))
        reserve_sb = sb.tile([P, 1], F32, name="reserve_sb")
        nc.sync.dma_start(out=reserve_sb[:], in_=reserve)
        old_sb = sb.tile([P, T], F32, name="old_sb")
        nc.sync.dma_start(out=old_sb[:], in_=old)

        placed = sb.tile([P, T], F32, name="placed")
        nc.vector.memset(placed[:], 0.0)
        th_wide = sb.tile([P, SLOTS], F32, name="th_wide")
        nc.gpsimd.tensor_scalar(th_wide[:], placed[:, :SLOTS], th_sb[:], 1.0, ALU.add, ALU.mult)
        half = sb.tile([P, 1], F32, name="half")
        nc.scalar.activation(half[:], placed[:, 0:1], ACT.Sigmoid)

        q_codes, q_scales = quantise(nc.vector.tensor_copy, q_raw, "q")
        g_codes, g_scales = quantise(nc.vector.tensor_copy, g_raw, "g")
        scores = sb.tile([P, T], F32, name="scores")
        for n, lo in enumerate(range(0, T, SCORE_N)):
            bank = psum.tile([P, 512], F32, name="bank")
            nc.tensor.matmul_mx(
                out=bank[:, :SCORE_N],
                lhsT=q_codes[:].bitcast(FP8X4),
                lhsT_scale=q_scales[:],
                rhs=key_words[:, 2 * lo : 2 * (lo + SCORE_N)].bitcast(FP4X4),
                rhs_scale=key_scales[:, lo : lo + SCORE_N],
                start=True,
                stop=True,
            )
            nc.scalar.copy(out=scores[:, lo : lo + SCORE_N], in_=bank[:, :SCORE_N])

        margin = sb.tile([P, SLOTS], F32, name="margin")
        sig = sb.tile([P, SLOTS], F32, name="sig")
        dist = sb.tile([P, SLOTS], F32, name="dist", tag="dist_grads")
        for lo in range(0, SLOTS, HALF):
            part = slice(lo, lo + HALF)
            listed = offsets[:, lo // 16 : (lo + HALF) // 16]
            nc.vector.tensor_tensor(margin[:, part], scores[:].indirect(listed), th_wide[:, part], ALU.subtract)
            nc.scalar.activation(sig[:, part], margin[:, part], ACT.Sigmoid)
            nc.scalar.activation(dist[:, part], sig[:, part], ACT.Abs, bias=half[:], scale=-1.0)
        log_sig = sb.tile([P, SLOTS], F32, name="log_sig")
        nc.scalar.activation(log_sig[:], dist[:], ACT.Ln, bias=half[:])

        grads = sb.tile([P, T], F32, name="grads", tag="dist_grads")
        for chunks in BANK_CHUNKS:
            bank = psum.tile([P, 512], F32, name="bank")
            first = starts[chunks[0]]
            for c in chunks:
                copy = nc.scalar.copy if c == 1 else nc.vector.tensor_copy
                v_codes, v_scales = quantise(copy, v_raw[c], "v%d" % c)
                nc.tensor.matmul_mx(
                    out=bank[:, starts[c] - first : starts[c] - first + VAL_CHUNKS[c]],
                    lhsT=g_codes[:].bitcast(FP8X4),
                    lhsT_scale=g_scales[:],
                    rhs=v_codes[:].bitcast(FP8X4),
                    rhs_scale=v_scales[:],
                    start=True,
                    stop=True,
                )
            width = sum(VAL_CHUNKS[c] for c in chunks)
            nc.scalar.copy(out=grads[:, first : first + width], in_=bank[:, :width])

        weight = sb.tile([P, SLOTS], F32, name="weight")
        weight_sum = sb.tile([P, 1], F32, name="weight_sum")
        nc.vector.scalar_tensor_tensor(
            weight[:], margin[:], 0.0, log_sig[:], ALU.max, ALU.subtract, accum_out=weight_sum[:]
        )
        neg_z = sb.tile([P, 1], F32, name="neg_z")
        nc.vector.tensor_scalar(neg_z[:], weight_sum[:], reserve_sb[:], -1.0, ALU.add, ALU.mult)
        neg_inv_z = sb.tile([P, 1], F32, name="neg_inv_z")
        nc.vector.reciprocal(neg_inv_z[:], neg_z[:])
        gain_z = sb.tile([P, 1], F32, name="gain_z")
        nc.scalar.activation(gain_z[:], neg_inv_z[:], ACT.Copy, scale=-GAIN)

        dw = sb.tile([P, SLOTS], F32, name="dw")
        nc.vector.tensor_copy(dw[:], grads[:].indirect(offsets[:]))
        terms = sb.tile([P, SLOTS], F32, name="terms")
        shift = sb.tile([P, 1], F32, name="shift")
        nc.vector.scalar_tensor_tensor(
            terms[:], dw[:], neg_inv_z[:], weight[:], ALU.mult, ALU.mult, accum_out=shift[:]
        )
        dp = sb.tile([P, SLOTS], F32, name="dp")
        nc.vector.tensor_scalar(dp[:], dw[:], shift[:], gain_z[:], ALU.add, ALU.mult)
        nc.vector.tensor_tensor(placed[:].indirect(offsets[:]), dp[:], sig[:], ALU.mult)

        lo = 0
        for n, width in enumerate(OUT_PIECES):
            piece = sb.tile([P, width], F32, name="piece%d" % n)
            nc.vector.tensor_tensor(piece[:], placed[:, lo : lo + width], old_sb[:, lo : lo + width], ALU.add)
            queue = nc.sync if n % 2 == 0 else nc.scalar
            queue.dma_start(out=out[:, lo : lo + width], in_=piece[:])
            lo = lo + width
